import numpy as np
import ml_dtypes


def mxq(x, axis, fmt="e4m3"):
    dtype, down = {"e4m3": (ml_dtypes.float8_e4m3fn, 7), "e5m2": (ml_dtypes.float8_e5m2, 14)}[fmt]
    v = np.moveaxis(np.asarray(x, np.float32).astype(ml_dtypes.bfloat16).astype(np.float64), axis, -1)
    blocks = v.reshape(v.shape[:-1] + (-1, 32))
    amax = np.abs(blocks).max(-1, keepdims=True)
    byte = np.maximum(np.where(amax > 0, np.frexp(amax)[1] - 1 + 127, 0) - down, 1)
    scale = np.exp2(byte - 127.0)
    codes = (blocks / scale).astype(np.float32).astype(dtype).astype(np.float64)
    return np.moveaxis((codes * scale).reshape(v.shape), -1, axis)


WIDE = False


def mx_kscale(k):
    if not WIDE:
        return np.ones(k)
    levels = np.array([10, -10, 5, -5, 0])
    if k % 512:
        return np.exp2(np.random.permutation(np.resize(levels, k // 32))).repeat(32)
    a = np.empty((k // 512, 16))
    for p in range(k // 512):
        a[p, :8] = np.random.permutation(np.resize(levels, 8))
        for g in range(8):
            far = levels[np.abs(levels - a[p, g]) >= 10]
            a[p, g + 8] = far[np.random.randint(len(far))]
    return np.exp2(a.ravel()).repeat(32)


def f64(x):
    return np.asarray(x).astype(np.float64)


def striped(idx):
    return np.tile(idx.reshape(-1, 16).T, (8, 1)).astype(np.uint16)


def unstriped(offs):
    return offs[:16].T.reshape(-1).astype(np.int64)


def pack_weight(w):
    k, n = w.shape
    w = f64(np.asarray(w, np.float32).astype(ml_dtypes.bfloat16)).reshape(k // 32, 32, n)
    amax = np.abs(w).max(1)
    byte = np.clip(np.where(amax > 0, np.frexp(amax)[1] - 1 + 127 - 7, 1), 1, 254)
    scaled = (w * np.exp2(127.0 - byte)[:, None, :]).reshape(k, n).astype(np.float32)
    words = np.ascontiguousarray(scaled.reshape(k // 512, 128, 4, n).transpose(0, 1, 3, 2)).astype(ml_dtypes.float8_e4m3fn).view(np.uint8)
    return words, np.ascontiguousarray(byte.astype(np.uint8).reshape(k // 512, 16, n))


def unpack_weight(words, scales):
    g, p, n, _ = words.shape
    vals = np.ascontiguousarray(words).view(ml_dtypes.float8_e4m3fn).astype(np.float64) * np.repeat(np.exp2(scales.astype(np.float64) - 127.0), 8, axis=1)[..., None]
    return vals.transpose(0, 1, 3, 2).reshape(g * 512, n)

def planes(y):
    n, m = y.shape
    v = y.astype(np.float32).astype(ml_dtypes.bfloat16).astype(np.float64).reshape(n // 32, 32, m)
    top = np.abs(v).max(1)
    byte = np.clip(np.where(top > 0, np.frexp(top)[1] - 1 + 127 - 7, 1), 1, 254)
    codes = (v * np.exp2(127.0 - byte)[:, None, :]).reshape(n, m).astype(np.float32).astype(ml_dtypes.float8_e4m3fn).view(np.uint8)
    words = codes.reshape(n // 512, 128, 4, m).transpose(0, 1, 3, 2)
    return np.ascontiguousarray(words), np.ascontiguousarray(byte.astype(np.uint8).reshape(n // 512, 16, m))


K, T, S, N, U = 512, 1024, 512, 512, 1024
P = 2 ** 7


def setup_inputs():
    n = np.random.standard_normal
    s = mx_kscale(K)[:, None]
    packed_xT = pack_weight(n((K, T)) * s)
    return {
        "x_words": packed_xT[0],
        "x_scales": packed_xT[1],
        "mem": n((N, U)).astype(np.float32),
        "w1": (n((K, N)) / np.sqrt(K) / s).astype(np.float32),
        "old": np.tile(np.random.uniform(0.5, 0.95, S), (P, 1)).astype(np.float32),
        "new": np.tile(np.random.uniform(0.05, 0.5, S), (P, 1)).astype(np.float32),
        "offs": striped(np.random.permutation(T)[:S]),
        "slot": striped(np.random.permutation(U)[:S]),
    }


def reference(x_words, x_scales, mem, w1, old, new, offs, slot):
    xq = unpack_weight(x_words, x_scales)[:, unstriped(offs)]
    y = mxq(f64(w1), 0, "e4m3").T @ xq
    out = f64(mem).copy()
    out[:, unstriped(slot)] = f64(mem)[:, unstriped(slot)] * f64(old)[:1] + y * f64(new)[:1]
    return (out,) + planes(out)

@@ -1,0 +1,142 @@
+from contextlib import ExitStack
+
+import concourse.mybir as mybir
+from concourse.masks import make_identity
+
+K, T, S, N, U = 512, 1024, 512, 512, 1024
+FLOPS = 2 * K * N * S
+
+F32 = mybir.dt.float32
+BF16 = mybir.dt.bfloat16
+I32 = mybir.dt.int32
+U32 = mybir.dt.uint32
+U16 = mybir.dt.uint16
+U8 = mybir.dt.uint8
+FP8X4 = mybir.dt.float8_e4m3fn_x4
+MULT = mybir.AluOpType.mult
+ADD = mybir.AluOpType.add
+COPY = mybir.ActivationFunctionType.Copy
+
+P = 128
+PACK = 4
+BLOCKS = S // P
+ORDER = (0, 2, 3, 1)
+PIECES = ((0, 512), (512, 768), (768, 1024))
+
+
+def tile_picked_ema_none_po_kernel(tc, x_words, x_scales, mem, w1, old, new, offs, slot, out_0, out_1, out_2):
+    nc = tc.nc
+    with ExitStack() as ctx:
+        sb = ctx.enter_context(tc.tile_pool(name="sb", bufs=1))
+        ps = ctx.enter_context(tc.psum_pool(name="ps", bufs=1))
+
+        offs_sb = sb.tile([P, S // 16], U16, name="offs_sb")
+        slot_sb = sb.tile([P, S // 16], U16, name="slot_sb")
+        xw = sb.tile([P, T], U32, name="xw", align_bytes=64)
+        xs = sb.tile([P, T], U8, name="xs", align_bytes=64)
+        xs_rows = sb.tile([P, T // 4], I32, name="xs_rows", align_bytes=64)
+        w_raw = [sb.tile([P, PACK, N // 2], F32, name=f"w_raw{h}", align_bytes=64) for h in range(2)]
+        rows = sb.tile([BLOCKS, P], F32, name="rows")
+        new_rows = sb.tile([P, P], F32, name="new_rows")
+        old_sb = sb.tile([P, S], F32, name="old_sb", align_bytes=64)
+        win = [sb.tile([P, U], F32, name=f"win{t}", align_bytes=64) for t in range(PACK)]
+        ident = sb.tile([P, P], F32, name="ident")
+
+        nc.vector.memset(new_rows[:], 0.0)
+        nc.vector.memset(xs[:].bitcast(I32), 0)
+        make_identity(nc, ident[:])
+
+        nc.sync.dma_start(offs_sb[:], offs)
+        nc.sync.dma_start(rows[:], new[0].rearrange("(b j) -> b j", j=P))
+        nc.sync.dma_start(xw[:].bitcast(I32), x_words[0].rearrange("p n t -> p (n t)").bitcast(I32))
+        for q in range(4):
+            nc.scalar.dma_start(xs_rows[32 * q : 32 * q + 4, :], x_scales[0, 4 * q : 4 * q + 4, :].bitcast(I32))
+        w_rows = w1.rearrange("(p j) c -> p j c", j=PACK)
+        for h in range(2):
+            nc.sync.dma_start(w_raw[h][:], w_rows[:, :, h * 256 : (h + 1) * 256])
+        nc.sync.dma_start(slot_sb[:], slot)
+        nc.sync.dma_start(old_sb[:], old)
+        mem_rows = mem.rearrange("(p t) c -> p t c", t=PACK)
+        out_rows = out_0.rearrange("(p t) c -> p t c", t=PACK)
+        for t in ORDER:
+            nc.sync.dma_start(win[t][:], mem_rows[:, t, :])
+
+        xw_g = sb.tile([P, S], U32, name="xw_g", align_bytes=64)
+        xs_g = sb.tile([P, S], U8, name="xs_g", align_bytes=64)
+        banks = [ps.tile([P, 512], F32, name=f"bank{b}") for b in range(8)]
+        new_cols = sb.tile([P, BLOCKS], F32, name="new_cols")
+        nc.vector.tensor_copy(new_rows[0:BLOCKS, :], rows[:])
+        nc.tensor.transpose(banks[7][:, 0:P], new_rows[:], ident[:])
+        nc.scalar.copy(new_cols[:], banks[7][:, 0:BLOCKS])
+
+        for q in range(4):
+            nc.vector.tensor_copy(xs[32 * q : 32 * q + 4, :].bitcast(I32), xs_rows[32 * q : 32 * q + 4, :])
+        nc.vector.tensor_copy(xs_g[:], xs[:].indirect(offs_sb[:]))
+        nc.vector.tensor_copy(xw_g[:], xw[:].indirect(offs_sb[:]))
+
+        w_codes = sb.tile([P, N], U32, name="w_codes", align_bytes=64)
+        w_scales = sb.tile([P, N], U8, name="w_scales", align_bytes=64)
+        w_bf = sb.tile([P, PACK, P, PACK], BF16, name="w_bf", tag="after_w", align_bytes=64)
+        dealt = [w_bf[:, :, h * 64 : (h + 1) * 64, :].rearrange("p t m j -> p m t j") for h in range(2)]
+        source = [w_raw[h][:].rearrange("p j (m t) -> p m t j", t=PACK) for h in range(2)]
+        nc.scalar.activation(dealt[0], source[0], COPY)
+        nc.vector.tensor_copy(dealt[1], source[1])
+        for lo, hi in ((0, 1), (2, 4), (1, 2)):
+            cols = slice(lo * P, hi * P)
+            nc.vector.quantize_mx(
+                out=w_codes[:, cols].bitcast(FP8X4),
+                scales=w_scales[:, cols],
+                in_=w_bf[:, lo:hi].rearrange("p t m j -> p (t m j)"),
+            )
+
+        y_t = [sb.tile([P, PACK, P], F32, name=f"y_t{b}", tag=f"shared{b}", align_bytes=64) for b in range(BLOCKS)]
+        y = [sb.tile([P, S], F32, name=f"y{n}", align_bytes=64) for n in range(PACK - 1)]
+        for n, t in enumerate(ORDER):
+            w_cols = slice(t * P, (t + 1) * P)
+            for b in range(BLOCKS):
+                cols = slice(b * P, (b + 1) * P)
+                nc.tensor.matmul_mx(
+                    out=banks[b][:, w_cols],
+                    lhsT=xw_g[:, cols].bitcast(FP8X4),
+                    lhsT_scale=xs_g[:, cols],
+                    rhs=w_codes[:, w_cols].bitcast(FP8X4),
+                    rhs_scale=w_scales[:, w_cols],
+                    start=True,
+                    stop=True,
+                )
+                nc.scalar.activation(y_t[b][:, t, :], banks[b][:, w_cols], COPY, scale=new_cols[:, b : b + 1])
+            for b in range(BLOCKS):
+                nc.tensor.transpose(banks[4 + n][:, b * P : (b + 1) * P], y_t[b][:, t, :], ident[:])
+            if n < PACK - 1:
+                nc.scalar.copy(y[n][:], banks[4 + n][:])
+
+        kept = sb.tile([P, PACK, S], F32, name="kept", tag="after_w", align_bytes=64)
+        for t in ORDER:
+            nc.vector.tensor_tensor(kept[:, t, :], win[t][:].indirect(slot_sb[:]), old_sb[:], MULT)
+
+        grouped = [
+            sb.tile([P, hi - lo, PACK], BF16, name=f"grouped{i}", tag=f"shared{BLOCKS - 1 - i}", align_bytes=64)
+            for i, (lo, hi) in enumerate(PIECES)
+        ]
+        for n, t in enumerate(ORDER):
+            nc.vector.tensor_tensor(win[t][:].indirect(slot_sb[:]), kept[:, t, :], y[n % (PACK - 1)][:], ADD)
+            nc.sync.dma_start(out_rows[:, t, :], win[t][:])
+            for i, (lo, hi) in enumerate(PIECES):
+                if t == ORDER[-1] and i == 0:
+                    nc.vector.tensor_copy(grouped[i][:, :, t], win[t][:, lo:hi])
+                else:
+                    nc.scalar.copy(grouped[i][:, :, t], win[t][:, lo:hi])
+            if n == 0:
+                nc.scalar.copy(y[0][:], banks[7][:])
+
+        o_codes = [sb.tile([P, hi - lo], U32, name=f"o_codes{lo}", align_bytes=64) for lo, hi in PIECES]
+        o_scales = sb.tile([P, U], U8, name="o_scales", align_bytes=64)
+        o_words = out_1[0].rearrange("p n t -> p (n t)").bitcast(I32)
+        for i in (1, 0, 2):
+            lo, hi = PIECES[i]
+            nc.vector.quantize_mx(
+                out=o_codes[i][:].bitcast(FP8X4), scales=o_scales[:, lo:hi], in_=grouped[i][:].rearrange("p c t -> p (c t)")
+            )
+            nc.sync.dma_start(o_words[:, lo:hi], o_codes[i][:].bitcast(I32))
+        for q in range(4):
+            nc.scalar.dma_start(out_2[0, 4 * q : 4 * q + 4, :].bitcast(I32), o_scales[32 * q : 32 * q + 4, :].bitcast(I32))

@@ -30,96 +30,113 @@ def tile_picked_ema_none_po_kernel(tc, x_words, x_scales, mem, w1, old, new, off
         sb = ctx.enter_context(tc.tile_pool(name="sb", bufs=1))
         ps = ctx.enter_context(tc.psum_pool(name="ps", bufs=1))
 
+        half = N // 2
         offs_sb = sb.tile([P, S // 16], U16, name="offs_sb")
         slot_sb = sb.tile([P, S // 16], U16, name="slot_sb")
         xw = sb.tile([P, T], U32, name="xw", align_bytes=64)
         xs = sb.tile([P, T], U8, name="xs", align_bytes=64)
         xs_rows = sb.tile([P, T // 4], I32, name="xs_rows", align_bytes=64)
-        w_raw = [sb.tile([P, PACK, N // 2], F32, name=f"w_raw{h}", align_bytes=64) for h in range(2)]
-        rows = sb.tile([BLOCKS, P], F32, name="rows")
-        new_rows = sb.tile([P, P], F32, name="new_rows")
+        w_raw = [sb.tile([P, PACK, half], F32, name=f"w_raw{h}", align_bytes=64) for h in range(2)]
+        new_rows = sb.tile([BLOCKS, P], F32, name="new_rows")
+        new_square = sb.tile([P, P], F32, name="new_square")
+        old_rows = sb.tile([BLOCKS, P], F32, name="old_rows")
+        old_square = sb.tile([P, P], F32, name="old_square")
         old_sb = sb.tile([P, S], F32, name="old_sb", align_bytes=64)
         win = [sb.tile([P, U], F32, name=f"win{t}", align_bytes=64) for t in range(PACK)]
         ident = sb.tile([P, P], F32, name="ident")
+        banks = [ps.tile([P, 512], F32, name=f"bank{b}") for b in range(8)]
 
-        nc.vector.memset(new_rows[:], 0.0)
         nc.vector.memset(xs[:].bitcast(I32), 0)
+        nc.vector.memset(old_square[:], 0.0)
+        nc.vector.memset(new_square[:], 0.0)
         make_identity(nc, ident[:])
 
         nc.sync.dma_start(offs_sb[:], offs)
-        nc.sync.dma_start(rows[:], new[0].rearrange("(b j) -> b j", j=P))
-        nc.sync.dma_start(xw[:].bitcast(I32), x_words[0].rearrange("p n t -> p (n t)").bitcast(I32))
         for q in range(4):
-            nc.scalar.dma_start(xs_rows[32 * q : 32 * q + 4, :], x_scales[0, 4 * q : 4 * q + 4, :].bitcast(I32))
+            queue = nc.sync if q < 2 else nc.scalar
+            queue.dma_start(xs_rows[32 * q : 32 * q + 4, :], x_scales[0, 4 * q : 4 * q + 4, :].bitcast(I32))
+        nc.scalar.dma_start(old_rows[:], old[0].rearrange("(b j) -> b j", j=P))
         w_rows = w1.rearrange("(p j) c -> p j c", j=PACK)
         for h in range(2):
-            nc.sync.dma_start(w_raw[h][:], w_rows[:, :, h * 256 : (h + 1) * 256])
+            nc.sync.dma_start(w_raw[h][:], w_rows[:, :, h * half : (h + 1) * half])
+        nc.sync.dma_start(new_rows[:], new[0].rearrange("(b j) -> b j", j=P))
+        nc.sync.dma_start(xw[:].bitcast(I32), x_words[0].rearrange("p n t -> p (n t)").bitcast(I32))
         nc.sync.dma_start(slot_sb[:], slot)
-        nc.sync.dma_start(old_sb[:], old)
         mem_rows = mem.rearrange("(p t) c -> p t c", t=PACK)
         out_rows = out_0.rearrange("(p t) c -> p t c", t=PACK)
         for t in ORDER:
             nc.sync.dma_start(win[t][:], mem_rows[:, t, :])
 
-        xw_g = sb.tile([P, S], U32, name="xw_g", align_bytes=64)
         xs_g = sb.tile([P, S], U8, name="xs_g", align_bytes=64)
-        banks = [ps.tile([P, 512], F32, name=f"bank{b}") for b in range(8)]
-        new_cols = sb.tile([P, BLOCKS], F32, name="new_cols")
-        nc.vector.tensor_copy(new_rows[0:BLOCKS, :], rows[:])
-        nc.tensor.transpose(banks[7][:, 0:P], new_rows[:], ident[:])
-        nc.scalar.copy(new_cols[:], banks[7][:, 0:BLOCKS])
-
         for q in range(4):
             nc.vector.tensor_copy(xs[32 * q : 32 * q + 4, :].bitcast(I32), xs_rows[32 * q : 32 * q + 4, :])
+        nc.vector.tensor_copy(old_square[0:BLOCKS, :], old_rows[:])
         nc.vector.tensor_copy(xs_g[:], xs[:].indirect(offs_sb[:]))
-        nc.vector.tensor_copy(xw_g[:], xw[:].indirect(offs_sb[:]))
+
+        old_cols = sb.tile([P, BLOCKS], F32, name="old_cols")
+        nc.tensor.transpose(banks[6][:, 0:P], old_square[:], ident[:])
+        nc.scalar.copy(old_cols[:], banks[6][:, 0:BLOCKS])
+        for b in range(BLOCKS):
+            nc.tensor.transpose(banks[b][:, 0:P], old_cols[:, b : b + 1].to_broadcast([P, P]), ident[:])
 
         w_codes = sb.tile([P, N], U32, name="w_codes", align_bytes=64)
         w_scales = sb.tile([P, N], U8, name="w_scales", align_bytes=64)
-        w_bf = sb.tile([P, PACK, P, PACK], BF16, name="w_bf", tag="after_w", align_bytes=64)
-        dealt = [w_bf[:, :, h * 64 : (h + 1) * 64, :].rearrange("p t m j -> p m t j") for h in range(2)]
-        source = [w_raw[h][:].rearrange("p j (m t) -> p m t j", t=PACK) for h in range(2)]
-        nc.scalar.activation(dealt[0], source[0], COPY)
-        nc.vector.tensor_copy(dealt[1], source[1])
-        for lo, hi in ((0, 1), (2, 4), (1, 2)):
-            cols = slice(lo * P, hi * P)
+        w_bf = [sb.tile([P, half, PACK], BF16, name=f"w_bf{h}", tag=f"after_w{h}", align_bytes=64) for h in range(2)]
+        woven = [bf[:].rearrange("p (c i) j -> p c j i", i=4) for bf in w_bf]
+        source = [raw[:].rearrange("p j (c i) -> p c j i", i=4) for raw in w_raw]
+        nc.scalar.activation(woven[0], source[0], COPY)
+        nc.vector.tensor_copy(woven[1], source[1])
+        for h in range(2):
+            cols = slice(h * half, (h + 1) * half)
             nc.vector.quantize_mx(
-                out=w_codes[:, cols].bitcast(FP8X4),
-                scales=w_scales[:, cols],
-                in_=w_bf[:, lo:hi].rearrange("p t m j -> p (t m j)"),
+                out=w_codes[:, cols].bitcast(FP8X4), scales=w_scales[:, cols], in_=w_bf[h][:].rearrange("p c j -> p (c j)")
             )
+        for b in range(BLOCKS):
+            nc.scalar.copy(old_sb[:, b * P : (b + 1) * P], banks[b][:, 0:P])
+
+        new_cols = sb.tile([P, BLOCKS], F32, name="new_cols")
+        nc.scalar.copy(new_square[0:BLOCKS, :], new_rows[:])
+        nc.tensor.transpose(banks[7][:, 0:P], new_square[:], ident[:])
+        nc.scalar.copy(new_cols[:], banks[7][:, 0:BLOCKS])
 
         y_t = [sb.tile([P, PACK, P], F32, name=f"y_t{b}", tag=f"shared{b}", align_bytes=64) for b in range(BLOCKS)]
         y = [sb.tile([P, S], F32, name=f"y{n}", align_bytes=64) for n in range(PACK - 1)]
+        xw_g = [sb.tile([P, P], U32, name=f"xw_g{b}", align_bytes=64) for b in range(BLOCKS)]
+        for b in range(BLOCKS):
+            cols = slice(b * P, (b + 1) * P)
+            nc.vector.tensor_copy(xw_g[b][:], xw[:].indirect(offs_sb[:, b * P // 16 : (b + 1) * P // 16]))
+            nc.tensor.matmul_mx(
+                out=banks[b][:],
+                lhsT=xw_g[b][:].bitcast(FP8X4),
+                lhsT_scale=xs_g[:, cols],
+                rhs=w_codes[:].bitcast(FP8X4),
+                rhs_scale=w_scales[:],
+                start=True,
+                stop=True,
+            )
         for n, t in enumerate(ORDER):
-            w_cols = slice(t * P, (t + 1) * P)
-            for b in range(BLOCKS):
-                cols = slice(b * P, (b + 1) * P)
-                nc.tensor.matmul_mx(
-                    out=banks[b][:, w_cols],
-                    lhsT=xw_g[:, cols].bitcast(FP8X4),
-                    lhsT_scale=xs_g[:, cols],
-                    rhs=w_codes[:, w_cols].bitcast(FP8X4),
-                    rhs_scale=w_scales[:, w_cols],
-                    start=True,
-                    stop=True,
-                )
-                nc.scalar.activation(y_t[b][:, t, :], banks[b][:, w_cols], COPY, scale=new_cols[:, b : b + 1])
+            if n < 2:
+                planes = slice(0, 1) if n == 0 else slice(1, PACK)
+                for b in range(BLOCKS):
+                    dealt = banks[b][:].rearrange("j (p t) -> j t p", t=PACK)
+                    nc.scalar.activation(y_t[b][:, planes, :], dealt[:, planes, :], COPY, scale=new_cols[:, b : b + 1])
             for b in range(BLOCKS):
                 nc.tensor.transpose(banks[4 + n][:, b * P : (b + 1) * P], y_t[b][:, t, :], ident[:])
             if n < PACK - 1:
                 nc.scalar.copy(y[n][:], banks[4 + n][:])
 
-        kept = sb.tile([P, PACK, S], F32, name="kept", tag="after_w", align_bytes=64)
-        for t in ORDER:
-            nc.vector.tensor_tensor(kept[:, t, :], win[t][:].indirect(slot_sb[:]), old_sb[:], MULT)
+        kept_first = sb.tile([P, PACK - 1, S], F32, name="kept_first", tag="after_w1", align_bytes=64)
+        kept_last = sb.tile([P, S], F32, name="kept_last", tag="shared0", align_bytes=64)
+        kept = [kept_first[:, n, :] for n in range(PACK - 1)] + [kept_last[:]]
+        for n, t in enumerate(ORDER):
+            nc.vector.tensor_tensor(kept[n], win[t][:].indirect(slot_sb[:]), old_sb[:], MULT)
 
         grouped = [
             sb.tile([P, hi - lo, PACK], BF16, name=f"grouped{i}", tag=f"shared{BLOCKS - 1 - i}", align_bytes=64)
             for i, (lo, hi) in enumerate(PIECES)
         ]
         for n, t in enumerate(ORDER):
-            nc.vector.tensor_tensor(win[t][:].indirect(slot_sb[:]), kept[:, t, :], y[n % (PACK - 1)][:], ADD)
+            nc.vector.tensor_tensor(win[t][:].indirect(slot_sb[:]), kept[n], y[n % (PACK - 1)][:], ADD)
             nc.sync.dma_start(out_rows[:, t, :], win[t][:])
             for i, (lo, hi) in enumerate(PIECES):
                 if t == ORDER[-1] and i == 0:
@@ -139,4 +156,5 @@ def tile_picked_ema_none_po_kernel(tc, x_words, x_scales, mem, w1, old, new, off
             )
             nc.sync.dma_start(o_words[:, lo:hi], o_codes[i][:].bitcast(I32))
         for q in range(4):
-            nc.scalar.dma_start(out_2[0, 4 * q : 4 * q + 4, :].bitcast(I32), o_scales[32 * q : 32 * q + 4, :].bitcast(I32))
+            queue = nc.scalar if q < 2 else nc.sync
+            queue.dma_start(out_2[0, 4 * q : 4 * q + 4, :].bitcast(I32), o_scales[32 * q : 32 * q + 4, :].bitcast(I32))

@@ -114,14 +114,18 @@ def tile_picked_ema_none_po_kernel(tc, x_words, x_scales, mem, w1, old, new, off
                 start=True,
                 stop=True,
             )
-        for n, t in enumerate(ORDER):
-            if n < 2:
-                planes = slice(0, 1) if n == 0 else slice(1, PACK)
-                for b in range(BLOCKS):
-                    dealt = banks[b][:].rearrange("j (p t) -> j t p", t=PACK)
-                    nc.scalar.activation(y_t[b][:, planes, :], dealt[:, planes, :], COPY, scale=new_cols[:, b : b + 1])
+        dealt = [banks[b][:].rearrange("j (p t) -> j t p", t=PACK) for b in range(BLOCKS)]
+        for pair in range(2):
+            for b in (2 * pair, 2 * pair + 1):
+                nc.scalar.activation(y_t[b][:, 0, :], dealt[b][:, 0, :], COPY, scale=new_cols[:, b : b + 1])
+                nc.tensor.transpose(banks[4][:, b * P : (b + 1) * P], y_t[b][:, 0, :], ident[:])
+            entries = slice(pair * S // 2, (pair + 1) * S // 2)
+            nc.scalar.copy(y[0][:, entries], banks[4][:, entries])
+        for b in range(BLOCKS):
+            nc.scalar.activation(y_t[b][:, 1:, :], dealt[b][:, 1:, :], COPY, scale=new_cols[:, b : b + 1])
+        for n in range(1, PACK):
             for b in range(BLOCKS):
-                nc.tensor.transpose(banks[4 + n][:, b * P : (b + 1) * P], y_t[b][:, t, :], ident[:])
+                nc.tensor.transpose(banks[4 + n][:, b * P : (b + 1) * P], y_t[b][:, ORDER[n], :], ident[:])
             if n < PACK - 1:
                 nc.scalar.copy(y[n][:], banks[4 + n][:])
 
@@ -136,7 +140,11 @@ def tile_picked_ema_none_po_kernel(tc, x_words, x_scales, mem, w1, old, new, off
             for i, (lo, hi) in enumerate(PIECES)
         ]
         for n, t in enumerate(ORDER):
-            nc.vector.tensor_tensor(win[t][:].indirect(slot_sb[:]), kept[n], y[n % (PACK - 1)][:], ADD)
+            parts = 2 if n == 0 else 1
+            for part in range(parts):
+                lo, hi = part * S // parts, (part + 1) * S // parts
+                places = win[t][:].indirect(slot_sb[:, lo // 16 : hi // 16])
+                nc.vector.tensor_tensor(places, kept[n][:, lo:hi], y[n % (PACK - 1)][:, lo:hi], ADD)
             nc.sync.dma_start(out_rows[:, t, :], win[t][:])
             for i, (lo, hi) in enumerate(PIECES):
                 if t == ORDER[-1] and i == 0:

@@ -1,7 +1,6 @@
 from contextlib import ExitStack
 
 import concourse.mybir as mybir
-from concourse.masks import make_identity
 
 K, T, S, N, U = 512, 1024, 512, 512, 1024
 FLOPS = 2 * K * N * S
@@ -19,9 +18,12 @@ COPY = mybir.ActivationFunctionType.Copy
 
 P = 128
 PACK = 4
-BLOCKS = S // P
-ORDER = (0, 2, 3, 1)
-PIECES = ((0, 512), (512, 768), (768, 1024))
+ORDER = (0, 1, 2, 3)
+HALF = S // 2
+W_FIRST = 80
+W_VECTOR = 32
+PIECES = ((0, 256, "scalar"), (256, 512, "vector"), (512, 704, "scalar"), (704, 1024, "vector"))
+QUANT = ((256, 512), (0, 256), (768, 1024), (512, 768))
 
 
 def tile_picked_ema_none_po_kernel(tc, x_words, x_scales, mem, w1, old, new, offs, slot, out_0, out_1, out_2):
@@ -30,139 +32,124 @@ def tile_picked_ema_none_po_kernel(tc, x_words, x_scales, mem, w1, old, new, off
         sb = ctx.enter_context(tc.tile_pool(name="sb", bufs=1))
         ps = ctx.enter_context(tc.psum_pool(name="ps", bufs=1))
 
-        half = N // 2
         offs_sb = sb.tile([P, S // 16], U16, name="offs_sb")
         slot_sb = sb.tile([P, S // 16], U16, name="slot_sb")
         xw = sb.tile([P, T], U32, name="xw", align_bytes=64)
         xs = sb.tile([P, T], U8, name="xs", align_bytes=64)
         xs_rows = sb.tile([P, T // 4], I32, name="xs_rows", align_bytes=64)
-        w_raw = [sb.tile([P, PACK, half], F32, name=f"w_raw{h}", align_bytes=64) for h in range(2)]
-        new_rows = sb.tile([BLOCKS, P], F32, name="new_rows")
-        new_square = sb.tile([P, P], F32, name="new_square")
-        old_rows = sb.tile([BLOCKS, P], F32, name="old_rows")
-        old_square = sb.tile([P, P], F32, name="old_square")
+        w_first = sb.tile([P, PACK, PACK * W_FIRST], F32, name="w_first", align_bytes=64)
+        w_rest = sb.tile([P, PACK, N - PACK * W_FIRST], F32, name="w_rest", align_bytes=64)
         old_sb = sb.tile([P, S], F32, name="old_sb", align_bytes=64)
+        new_sb = sb.tile([P, S], F32, name="new_sb", align_bytes=64)
         win = [sb.tile([P, U], F32, name=f"win{t}", align_bytes=64) for t in range(PACK)]
-        ident = sb.tile([P, P], F32, name="ident")
-        banks = [ps.tile([P, 512], F32, name=f"bank{b}") for b in range(8)]
+        banks = [ps.tile([P, S], F32, name=f"bank{t}") for t in range(PACK)]
 
         nc.vector.memset(xs[:].bitcast(I32), 0)
-        nc.vector.memset(old_square[:], 0.0)
-        nc.vector.memset(new_square[:], 0.0)
-        make_identity(nc, ident[:])
-
         nc.sync.dma_start(offs_sb[:], offs)
         for q in range(4):
             queue = nc.sync if q < 2 else nc.scalar
             queue.dma_start(xs_rows[32 * q : 32 * q + 4, :], x_scales[0, 4 * q : 4 * q + 4, :].bitcast(I32))
-        nc.scalar.dma_start(old_rows[:], old[0].rearrange("(b j) -> b j", j=P))
         w_rows = w1.rearrange("(p j) c -> p j c", j=PACK)
-        for h in range(2):
-            nc.sync.dma_start(w_raw[h][:], w_rows[:, :, h * half : (h + 1) * half])
-        nc.sync.dma_start(new_rows[:], new[0].rearrange("(b j) -> b j", j=P))
-        nc.sync.dma_start(xw[:].bitcast(I32), x_words[0].rearrange("p n t -> p (n t)").bitcast(I32))
-        nc.sync.dma_start(slot_sb[:], slot)
         mem_rows = mem.rearrange("(p t) c -> p t c", t=PACK)
         out_rows = out_0.rearrange("(p t) c -> p t c", t=PACK)
-        for t in ORDER:
+        nc.sync.dma_start(w_first[:], w_rows[:, :, : PACK * W_FIRST])
+        nc.sync.dma_start(xw[:].bitcast(I32), x_words[0].rearrange("p n t -> p (n t)").bitcast(I32))
+        nc.sync.dma_start(w_rest[:], w_rows[:, :, PACK * W_FIRST :])
+        nc.sync.dma_start(slot_sb[:], slot)
+        nc.sync.dma_start(win[0][:], mem_rows[:, 0, :])
+        nc.sync.dma_start(new_sb[:], new)
+        nc.sync.dma_start(old_sb[:], old)
+        for t in range(1, PACK):
             nc.sync.dma_start(win[t][:], mem_rows[:, t, :])
 
         xs_g = sb.tile([P, S], U8, name="xs_g", align_bytes=64)
+        xw_g = sb.tile([P, S], U32, name="xw_g", align_bytes=64)
         for q in range(4):
             nc.vector.tensor_copy(xs[32 * q : 32 * q + 4, :].bitcast(I32), xs_rows[32 * q : 32 * q + 4, :])
-        nc.vector.tensor_copy(old_square[0:BLOCKS, :], old_rows[:])
         nc.vector.tensor_copy(xs_g[:], xs[:].indirect(offs_sb[:]))
+        nc.vector.tensor_copy(xw_g[:], xw[:].indirect(offs_sb[:]))
 
-        old_cols = sb.tile([P, BLOCKS], F32, name="old_cols")
-        nc.tensor.transpose(banks[6][:, 0:P], old_square[:], ident[:])
-        nc.scalar.copy(old_cols[:], banks[6][:, 0:BLOCKS])
-        for b in range(BLOCKS):
-            nc.tensor.transpose(banks[b][:, 0:P], old_cols[:, b : b + 1].to_broadcast([P, P]), ident[:])
+        w_bf = sb.tile([P, PACK, P, PACK], BF16, name="w_bf", align_bytes=64)
 
-        w_codes = sb.tile([P, N], U32, name="w_codes", align_bytes=64)
-        w_scales = sb.tile([P, N], U8, name="w_scales", align_bytes=64)
-        w_bf = [sb.tile([P, half, PACK], BF16, name=f"w_bf{h}", tag=f"after_w{h}", align_bytes=64) for h in range(2)]
-        woven = [bf[:].rearrange("p (c i) j -> p c j i", i=4) for bf in w_bf]
-        source = [raw[:].rearrange("p j (c i) -> p c j i", i=4) for raw in w_raw]
-        nc.scalar.activation(woven[0], source[0], COPY)
-        nc.vector.tensor_copy(woven[1], source[1])
-        for h in range(2):
-            cols = slice(h * half, (h + 1) * half)
-            nc.vector.quantize_mx(
-                out=w_codes[:, cols].bitcast(FP8X4), scales=w_scales[:, cols], in_=w_bf[h][:].rearrange("p c j -> p (c j)")
-            )
-        for b in range(BLOCKS):
-            nc.scalar.copy(old_sb[:, b * P : (b + 1) * P], banks[b][:, 0:P])
+        def deal(raw, first, lo, hi):
+            dealt = w_bf[:, :, lo:hi, :].rearrange("p t m j -> p m t j")
+            source = raw[:, :, PACK * (lo - first) : PACK * (hi - first)].rearrange("p j (m t) -> p m t j", t=PACK)
+            return dealt, source
 
-        new_cols = sb.tile([P, BLOCKS], F32, name="new_cols")
-        nc.scalar.copy(new_square[0:BLOCKS, :], new_rows[:])
-        nc.tensor.transpose(banks[7][:, 0:P], new_square[:], ident[:])
-        nc.scalar.copy(new_cols[:], banks[7][:, 0:BLOCKS])
-
-        y_t = [sb.tile([P, PACK, P], F32, name=f"y_t{b}", tag=f"shared{b}", align_bytes=64) for b in range(BLOCKS)]
-        y = [sb.tile([P, S], F32, name=f"y{n}", align_bytes=64) for n in range(PACK - 1)]
-        xw_g = [sb.tile([P, P], U32, name=f"xw_g{b}", align_bytes=64) for b in range(BLOCKS)]
-        for b in range(BLOCKS):
-            cols = slice(b * P, (b + 1) * P)
-            nc.vector.tensor_copy(xw_g[b][:], xw[:].indirect(offs_sb[:, b * P // 16 : (b + 1) * P // 16]))
+        nc.scalar.activation(*deal(w_first, 0, 0, W_FIRST), COPY)
+        nc.vector.tensor_copy(*deal(w_rest, W_FIRST, W_FIRST, W_FIRST + W_VECTOR))
+        nc.scalar.activation(*deal(w_rest, W_FIRST, W_FIRST + W_VECTOR, P), COPY)
+        for t in range(PACK):
+            w_codes = sb.tile([P, P], U32, name=f"w_codes{t}", align_bytes=64)
+            w_scales = sb.tile([P, P], U8, name=f"w_scales{t}", align_bytes=64)
+            nc.vector.quantize_mx(out=w_codes[:].bitcast(FP8X4), scales=w_scales[:], in_=w_bf[:, t, :, :].rearrange("p m j -> p (m j)"))
             nc.tensor.matmul_mx(
-                out=banks[b][:],
-                lhsT=xw_g[b][:].bitcast(FP8X4),
-                lhsT_scale=xs_g[:, cols],
-                rhs=w_codes[:].bitcast(FP8X4),
-                rhs_scale=w_scales[:],
+                out=banks[t][:],
+                lhsT=w_codes[:].bitcast(FP8X4),
+                lhsT_scale=w_scales[:],
+                rhs=xw_g[:].bitcast(FP8X4),
+                rhs_scale=xs_g[:],
                 start=True,
                 stop=True,
             )
-        dealt = [banks[b][:].rearrange("j (p t) -> j t p", t=PACK) for b in range(BLOCKS)]
-        for pair in range(2):
-            for b in (2 * pair, 2 * pair + 1):
-                nc.scalar.activation(y_t[b][:, 0, :], dealt[b][:, 0, :], COPY, scale=new_cols[:, b : b + 1])
-                nc.tensor.transpose(banks[4][:, b * P : (b + 1) * P], y_t[b][:, 0, :], ident[:])
-            entries = slice(pair * S // 2, (pair + 1) * S // 2)
-            nc.scalar.copy(y[0][:, entries], banks[4][:, entries])
-        for b in range(BLOCKS):
-            nc.scalar.activation(y_t[b][:, 1:, :], dealt[b][:, 1:, :], COPY, scale=new_cols[:, b : b + 1])
-        for n in range(1, PACK):
-            for b in range(BLOCKS):
-                nc.tensor.transpose(banks[4 + n][:, b * P : (b + 1) * P], y_t[b][:, ORDER[n], :], ident[:])
-            if n < PACK - 1:
-                nc.scalar.copy(y[n][:], banks[4 + n][:])
 
-        kept_first = sb.tile([P, PACK - 1, S], F32, name="kept_first", tag="after_w1", align_bytes=64)
-        kept_last = sb.tile([P, S], F32, name="kept_last", tag="shared0", align_bytes=64)
-        kept = [kept_first[:, n, :] for n in range(PACK - 1)] + [kept_last[:]]
-        for n, t in enumerate(ORDER):
-            nc.vector.tensor_tensor(kept[n], win[t][:].indirect(slot_sb[:]), old_sb[:], MULT)
+        def places(t, lo, hi):
+            return win[t][:].indirect(slot_sb[:, lo // 16 : hi // 16])
 
-        grouped = [
-            sb.tile([P, hi - lo, PACK], BF16, name=f"grouped{i}", tag=f"shared{BLOCKS - 1 - i}", align_bytes=64)
-            for i, (lo, hi) in enumerate(PIECES)
-        ]
-        for n, t in enumerate(ORDER):
-            parts = 2 if n == 0 else 1
-            for part in range(parts):
-                lo, hi = part * S // parts, (part + 1) * S // parts
-                places = win[t][:].indirect(slot_sb[:, lo // 16 : hi // 16])
-                nc.vector.tensor_tensor(places, kept[n][:, lo:hi], y[n % (PACK - 1)][:, lo:hi], ADD)
-            nc.sync.dma_start(out_rows[:, t, :], win[t][:])
-            for i, (lo, hi) in enumerate(PIECES):
-                if t == ORDER[-1] and i == 0:
-                    nc.vector.tensor_copy(grouped[i][:, :, t], win[t][:, lo:hi])
+        planes = [sb.tile([P, PACK, U // 2], F32, name=f"planes{h}", align_bytes=64) for h in range(2)]
+        picked = sb.tile([P, S], F32, name="picked", align_bytes=64)
+        for lo in (0, HALF):
+            nc.scalar.activation(picked[:, lo : lo + HALF], places(0, lo, lo + HALF), COPY)
+        fresh = [sb.tile([P, S], F32, name=f"fresh{t}", tag=f"fresh{t % 2}", align_bytes=64) for t in range(PACK)]
+
+        def weigh_new(t):
+            nc.vector.tensor_tensor(fresh[t][:], banks[t][:], new_sb[:], MULT)
+
+        weigh_new(0)
+        weigh_new(1)
+        for t in range(PACK):
+            last = t == PACK - 1
+            z = None if last else sb.tile([P, S], F32, name=f"z{t}", align_bytes=64)
+            kept = sb.tile([P, S], F32, name=f"kept{t}", tag="kept", align_bytes=64)
+            parts = ((0, HALF), (HALF, S)) if t == 0 else ((0, S),)
+            for lo, hi in parts:
+                looked_up = picked[:, lo:hi] if t == 0 else places(t, lo, hi)
+                nc.vector.tensor_tensor(kept[:, lo:hi], looked_up, old_sb[:, lo:hi], MULT)
+            if t in (1, 2):
+                weigh_new(t + 1)
+            for lo, hi in parts:
+                nc.vector.tensor_tensor(places(t, lo, hi) if last else z[:, lo:hi], kept[:, lo:hi], fresh[t][:, lo:hi], ADD)
+            if not last:
+                for lo in (0, HALF):
+                    nc.scalar.activation(places(t, lo, lo + HALF), z[:, lo : lo + HALF], COPY)
+            for h in range(2):
+                columns = win[t][:, h * U // 2 : (h + 1) * U // 2]
+                if t < 2:
+                    nc.sync.dma_start(planes[h][:, t, :], columns)
+                elif last:
+                    nc.vector.tensor_copy(planes[h][:, t, :], columns)
                 else:
-                    nc.scalar.copy(grouped[i][:, :, t], win[t][:, lo:hi])
-            if n == 0:
-                nc.scalar.copy(y[0][:], banks[7][:])
+                    nc.scalar.copy(planes[h][:, t, :], columns)
+            nc.sync.dma_start(out_rows[:, t, :], win[t][:])
 
-        o_codes = [sb.tile([P, hi - lo], U32, name=f"o_codes{lo}", align_bytes=64) for lo, hi in PIECES]
         o_scales = sb.tile([P, U], U8, name="o_scales", align_bytes=64)
         o_words = out_1[0].rearrange("p n t -> p (n t)").bitcast(I32)
-        for i in (1, 0, 2):
-            lo, hi = PIECES[i]
-            nc.vector.quantize_mx(
-                out=o_codes[i][:].bitcast(FP8X4), scales=o_scales[:, lo:hi], in_=grouped[i][:].rearrange("p c t -> p (c t)")
-            )
-            nc.sync.dma_start(o_words[:, lo:hi], o_codes[i][:].bitcast(I32))
+        grouped = [sb.tile([P, U // 2, PACK], BF16, name=f"grouped{h}", align_bytes=64) for h in range(2)]
+        for lo, hi, engine in PIECES:
+            h = lo // (U // 2)
+            cols = slice(lo - h * U // 2, hi - h * U // 2)
+            source = planes[h][:, :, cols].rearrange("p t (c i) -> p c t i", i=4)
+            woven = grouped[h][:, cols, :].rearrange("p (c i) t -> p c t i", i=4)
+            if engine == "vector":
+                nc.vector.tensor_copy(woven, source)
+            else:
+                nc.scalar.activation(woven, source, COPY)
+        for lo, hi in QUANT:
+            h = lo // (U // 2)
+            cols = slice(lo - h * U // 2, hi - h * U // 2)
+            o_codes = sb.tile([P, hi - lo], U32, name=f"o_codes{lo}", align_bytes=64)
+            nc.vector.quantize_mx(out=o_codes[:].bitcast(FP8X4), scales=o_scales[:, lo:hi], in_=grouped[h][:, cols, :].rearrange("p c t -> p (c t)"))
+            nc.sync.dma_start(o_words[:, lo:hi], o_codes[:].bitcast(I32))
         for q in range(4):
             queue = nc.scalar if q < 2 else nc.sync
             queue.dma_start(out_2[0, 4 * q : 4 * q + 4, :].bitcast(I32), o_scales[32 * q : 32 * q + 4, :].bitcast(I32))

@@ -20,6 +20,7 @@ P = 128
 PACK = 4
 ORDER = (0, 1, 2, 3)
 HALF = S // 2
+OWN = 128
 W_FIRST = 80
 W_VECTOR = 32
 PIECES = ((0, 256, "scalar"), (256, 512, "vector"), (512, 704, "scalar"), (704, 1024, "vector"))
@@ -117,11 +118,17 @@ def tile_picked_ema_none_po_kernel(tc, x_words, x_scales, mem, w1, old, new, off
                 nc.vector.tensor_tensor(kept[:, lo:hi], looked_up, old_sb[:, lo:hi], MULT)
             if t in (1, 2):
                 weigh_new(t + 1)
-            for lo, hi in parts:
-                nc.vector.tensor_tensor(places(t, lo, hi) if last else z[:, lo:hi], kept[:, lo:hi], fresh[t][:, lo:hi], ADD)
+            own = (0, 0, OWN, S)[t]
+            if t == 2:
+                parts = ((OWN, S),)
             if not last:
-                for lo in (0, HALF):
-                    nc.scalar.activation(places(t, lo, lo + HALF), z[:, lo : lo + HALF], COPY)
+                for lo, hi in parts:
+                    nc.vector.tensor_tensor(z[:, lo:hi], kept[:, lo:hi], fresh[t][:, lo:hi], ADD)
+            if own:
+                nc.vector.tensor_tensor(places(t, 0, own), kept[:, :own], fresh[t][:, :own], ADD)
+            if not last:
+                for lo, hi in parts if t == 2 else ((0, HALF), (HALF, S)):
+                    nc.scalar.activation(places(t, lo, hi), z[:, lo:hi], COPY)
             for h in range(2):
                 columns = win[t][:, h * U // 2 : (h + 1) * U // 2]
                 if t < 2:

@@ -20,7 +20,7 @@ P = 128
 PACK = 4
 ORDER = (0, 1, 2, 3)
 HALF = S // 2
-OWN = 128
+OWN = 64
 W_FIRST = 80
 W_VECTOR = 32
 PIECES = ((0, 256, "scalar"), (256, 512, "vector"), (512, 704, "scalar"), (704, 1024, "vector"))
@@ -127,7 +127,7 @@ def tile_picked_ema_none_po_kernel(tc, x_words, x_scales, mem, w1, old, new, off
             if own:
                 nc.vector.tensor_tensor(places(t, 0, own), kept[:, :own], fresh[t][:, :own], ADD)
             if not last:
-                for lo, hi in parts if t == 2 else ((0, HALF), (HALF, S)):
+                for lo, hi in ((own, own + (S - own) // 2), (own + (S - own) // 2, S)):
                     nc.scalar.activation(places(t, lo, hi), z[:, lo:hi], COPY)
             for h in range(2):
                 columns = win[t][:, h * U // 2 : (h + 1) * U // 2]

@@ -18,9 +18,7 @@ COPY = mybir.ActivationFunctionType.Copy
 
 P = 128
 PACK = 4
-ORDER = (0, 1, 2, 3)
 HALF = S // 2
-OWN = 64
 W_FIRST = 80
 W_VECTOR = 32
 PIECES = ((0, 256, "scalar"), (256, 512, "vector"), (512, 704, "scalar"), (704, 1024, "vector"))
@@ -39,11 +37,13 @@ def tile_picked_ema_none_po_kernel(tc, x_words, x_scales, mem, w1, old, new, off
         xs = sb.tile([P, T], U8, name="xs", align_bytes=64)
         xs_rows = sb.tile([P, T // 4], I32, name="xs_rows", align_bytes=64)
         w_first = sb.tile([P, PACK, PACK * W_FIRST], F32, name="w_first", align_bytes=64)
-        w_rest = sb.tile([P, PACK, N - PACK * W_FIRST], F32, name="w_rest", align_bytes=64)
+        w_rest = sb.tile([P, PACK, N - PACK * W_FIRST], F32, name="w_rest", tag="w_rest", align_bytes=64)
         old_sb = sb.tile([P, S], F32, name="old_sb", align_bytes=64)
         new_sb = sb.tile([P, S], F32, name="new_sb", align_bytes=64)
+        halves = ((0, HALF), (HALF, S))
         win = [sb.tile([P, U], F32, name=f"win{t}", align_bytes=64) for t in range(PACK)]
         banks = [ps.tile([P, S], F32, name=f"bank{t}") for t in range(PACK)]
+        first_bank = ps.tile([P, HALF], F32, name="first_bank")
 
         nc.vector.memset(xs[:].bitcast(I32), 0)
         nc.sync.dma_start(offs_sb[:], offs)
@@ -58,17 +58,18 @@ def tile_picked_ema_none_po_kernel(tc, x_words, x_scales, mem, w1, old, new, off
         nc.sync.dma_start(w_rest[:], w_rows[:, :, PACK * W_FIRST :])
         nc.sync.dma_start(slot_sb[:], slot)
         nc.sync.dma_start(win[0][:], mem_rows[:, 0, :])
-        nc.sync.dma_start(new_sb[:], new)
-        nc.sync.dma_start(old_sb[:], old)
+        for lo, hi in halves:
+            nc.sync.dma_start(new_sb[:, lo:hi], new[:, lo:hi])
+            nc.sync.dma_start(old_sb[:, lo:hi], old[:, lo:hi])
         for t in range(1, PACK):
             nc.sync.dma_start(win[t][:], mem_rows[:, t, :])
 
         xs_g = sb.tile([P, S], U8, name="xs_g", align_bytes=64)
-        xw_g = sb.tile([P, S], U32, name="xw_g", align_bytes=64)
+        xw_g = [sb.tile([P, HALF], U32, name="xw_g0", align_bytes=64)]
         for q in range(4):
             nc.vector.tensor_copy(xs[32 * q : 32 * q + 4, :].bitcast(I32), xs_rows[32 * q : 32 * q + 4, :])
         nc.vector.tensor_copy(xs_g[:], xs[:].indirect(offs_sb[:]))
-        nc.vector.tensor_copy(xw_g[:], xw[:].indirect(offs_sb[:]))
+        nc.vector.tensor_copy(xw_g[0][:], xw[:].indirect(offs_sb[:, : HALF // 16]))
 
         w_bf = sb.tile([P, PACK, P, PACK], BF16, name="w_bf", align_bytes=64)
 
@@ -80,47 +81,63 @@ def tile_picked_ema_none_po_kernel(tc, x_words, x_scales, mem, w1, old, new, off
         nc.scalar.activation(*deal(w_first, 0, 0, W_FIRST), COPY)
         nc.vector.tensor_copy(*deal(w_rest, W_FIRST, W_FIRST, W_FIRST + W_VECTOR))
         nc.scalar.activation(*deal(w_rest, W_FIRST, W_FIRST + W_VECTOR, P), COPY)
-        for t in range(PACK):
-            w_codes = sb.tile([P, P], U32, name=f"w_codes{t}", align_bytes=64)
-            w_scales = sb.tile([P, P], U8, name=f"w_scales{t}", align_bytes=64)
-            nc.vector.quantize_mx(out=w_codes[:].bitcast(FP8X4), scales=w_scales[:], in_=w_bf[:, t, :, :].rearrange("p m j -> p (m j)"))
+        w_codes = [sb.tile([P, P], U32, name=f"w_codes{t}", align_bytes=64) for t in range(PACK)]
+        w_scales = [sb.tile([P, P], U8, name=f"w_scales{t}", align_bytes=64) for t in range(PACK)]
+
+        def product(t, h):
+            lo, hi = halves[h]
             nc.tensor.matmul_mx(
-                out=banks[t][:],
-                lhsT=w_codes[:].bitcast(FP8X4),
-                lhsT_scale=w_scales[:],
-                rhs=xw_g[:].bitcast(FP8X4),
-                rhs_scale=xs_g[:],
+                out=first_bank[:] if (t, h) == (0, 0) else banks[t][:, lo:hi],
+                lhsT=w_codes[t][:].bitcast(FP8X4),
+                lhsT_scale=w_scales[t][:],
+                rhs=xw_g[h][:].bitcast(FP8X4),
+                rhs_scale=xs_g[:, lo:hi],
                 start=True,
                 stop=True,
             )
+
+        for t in range(PACK):
+            nc.vector.quantize_mx(out=w_codes[t][:].bitcast(FP8X4), scales=w_scales[t][:], in_=w_bf[:, t, :, :].rearrange("p m j -> p (m j)"))
+            product(t, 0)
+        xw_g.append(sb.tile([P, HALF], U32, name="xw_g1", tag="w_rest", align_bytes=64))
+        nc.vector.tensor_copy(xw_g[1][:], xw[:].indirect(offs_sb[:, HALF // 16 :]))
+        for t in range(PACK):
+            product(t, 1)
 
         def places(t, lo, hi):
             return win[t][:].indirect(slot_sb[:, lo // 16 : hi // 16])
 
         planes = [sb.tile([P, PACK, U // 2], F32, name=f"planes{h}", align_bytes=64) for h in range(2)]
-        picked = sb.tile([P, S], F32, name="picked", align_bytes=64)
-        for lo in (0, HALF):
-            nc.scalar.activation(picked[:, lo : lo + HALF], places(0, lo, lo + HALF), COPY)
+        picked = [sb.tile([P, HALF], F32, name=f"picked{h}", align_bytes=64) for h in range(2)]
+        for h, (lo, hi) in enumerate(halves):
+            nc.scalar.activation(picked[h][:], places(0, lo, hi), COPY)
         fresh = [sb.tile([P, S], F32, name=f"fresh{t}", tag=f"fresh{t % 2}", align_bytes=64) for t in range(PACK)]
 
         def weigh_new(t):
             nc.vector.tensor_tensor(fresh[t][:], banks[t][:], new_sb[:], MULT)
 
-        weigh_new(0)
-        weigh_new(1)
         for t in range(PACK):
             last = t == PACK - 1
             z = None if last else sb.tile([P, S], F32, name=f"z{t}", align_bytes=64)
-            kept = sb.tile([P, S], F32, name=f"kept{t}", tag="kept", align_bytes=64)
-            parts = ((0, HALF), (HALF, S)) if t == 0 else ((0, S),)
-            for lo, hi in parts:
-                looked_up = picked[:, lo:hi] if t == 0 else places(t, lo, hi)
-                nc.vector.tensor_tensor(kept[:, lo:hi], looked_up, old_sb[:, lo:hi], MULT)
+            kept = sb.tile([P, S], F32, name=f"kept{t}", align_bytes=64)
+            parts = ((0, S),)
+            if t == 0:
+                for h, (lo, hi) in enumerate(halves):
+                    nc.vector.tensor_tensor(kept[:, lo:hi], picked[h][:], old_sb[:, lo:hi], MULT)
+                    nc.vector.tensor_tensor(fresh[0][:, lo:hi], first_bank[:] if h == 0 else banks[0][:, lo:hi], new_sb[:, lo:hi], MULT)
+                    nc.vector.tensor_tensor(z[:, lo:hi], kept[:, lo:hi], fresh[0][:, lo:hi], ADD)
+                weigh_new(1)
+                parts = ()
+            elif t == 1:
+                for lo, hi in halves:
+                    nc.vector.tensor_tensor(kept[:, lo:hi], places(t, lo, hi), old_sb[:, lo:hi], MULT)
+                nc.vector.tensor_tensor(z[:, :HALF], kept[:, :HALF], fresh[t][:, :HALF], ADD)
+                parts = ((HALF, S),)
+            else:
+                nc.vector.tensor_tensor(kept[:], places(t, 0, S), old_sb[:], MULT)
             if t in (1, 2):
                 weigh_new(t + 1)
-            own = (0, 0, OWN, S)[t]
-            if t == 2:
-                parts = ((OWN, S),)
+            own = (0, 0, 0, S)[t]
             if not last:
                 for lo, hi in parts:
                     nc.vector.tensor_tensor(z[:, lo:hi], kept[:, lo:hi], fresh[t][:, lo:hi], ADD)

@@ -19,8 +19,7 @@ COPY = mybir.ActivationFunctionType.Copy
 P = 128
 PACK = 4
 HALF = S // 2
-W_FIRST = 80
-W_VECTOR = 32
+W_VECTOR = (76, 64)
 PIECES = ((0, 256, "scalar"), (256, 512, "vector"), (512, 704, "scalar"), (704, 1024, "vector"))
 QUANT = ((256, 512), (0, 256), (768, 1024), (512, 768))
 
@@ -35,9 +34,7 @@ def tile_picked_ema_none_po_kernel(tc, x_words, x_scales, mem, w1, old, new, off
         slot_sb = sb.tile([P, S // 16], U16, name="slot_sb")
         xw = sb.tile([P, T], U32, name="xw", align_bytes=64)
         xs = sb.tile([P, T], U8, name="xs", align_bytes=64)
-        xs_rows = sb.tile([P, T // 4], I32, name="xs_rows", align_bytes=64)
-        w_first = sb.tile([P, PACK, PACK * W_FIRST], F32, name="w_first", align_bytes=64)
-        w_rest = sb.tile([P, PACK, N - PACK * W_FIRST], F32, name="w_rest", tag="w_rest", align_bytes=64)
+        w_raw = sb.tile([P, PACK, N], F32, name="w_raw", align_bytes=64)
         old_sb = sb.tile([P, S], F32, name="old_sb", align_bytes=64)
         new_sb = sb.tile([P, S], F32, name="new_sb", align_bytes=64)
         halves = ((0, HALF), (HALF, S))
@@ -46,17 +43,16 @@ def tile_picked_ema_none_po_kernel(tc, x_words, x_scales, mem, w1, old, new, off
         first_bank = ps.tile([P, HALF], F32, name="first_bank")
 
         nc.vector.memset(xs[:].bitcast(I32), 0)
-        nc.sync.dma_start(offs_sb[:], offs)
-        for q in range(4):
-            queue = nc.sync if q < 2 else nc.scalar
-            queue.dma_start(xs_rows[32 * q : 32 * q + 4, :], x_scales[0, 4 * q : 4 * q + 4, :].bitcast(I32))
         w_rows = w1.rearrange("(p j) c -> p j c", j=PACK)
         mem_rows = mem.rearrange("(p t) c -> p t c", t=PACK)
         out_rows = out_0.rearrange("(p t) c -> p t c", t=PACK)
-        nc.sync.dma_start(w_first[:], w_rows[:, :, : PACK * W_FIRST])
         nc.sync.dma_start(xw[:].bitcast(I32), x_words[0].rearrange("p n t -> p (n t)").bitcast(I32))
-        nc.sync.dma_start(w_rest[:], w_rows[:, :, PACK * W_FIRST :])
+        nc.sync.dma_start(offs_sb[:], offs)
         nc.sync.dma_start(slot_sb[:], slot)
+        for q in range(4):
+            queue = nc.sync if q < 2 else nc.scalar
+            queue.dma_start(xs[32 * q : 32 * q + 4, :].bitcast(I32), x_scales[0, 4 * q : 4 * q + 4, :].bitcast(I32))
+        nc.sync.dma_start(w_raw[:], w_rows)
         nc.sync.dma_start(win[0][:], mem_rows[:, 0, :])
         for lo, hi in halves:
             nc.sync.dma_start(new_sb[:, lo:hi], new[:, lo:hi])
@@ -65,44 +61,41 @@ def tile_picked_ema_none_po_kernel(tc, x_words, x_scales, mem, w1, old, new, off
             nc.sync.dma_start(win[t][:], mem_rows[:, t, :])
 
         xs_g = sb.tile([P, S], U8, name="xs_g", align_bytes=64)
-        xw_g = [sb.tile([P, HALF], U32, name="xw_g0", align_bytes=64)]
-        for q in range(4):
-            nc.vector.tensor_copy(xs[32 * q : 32 * q + 4, :].bitcast(I32), xs_rows[32 * q : 32 * q + 4, :])
+        xw_g = sb.tile([P, S], U32, name="xw_g", align_bytes=64)
+        nc.vector.tensor_copy(xw_g[:], xw[:].indirect(offs_sb[:]))
         nc.vector.tensor_copy(xs_g[:], xs[:].indirect(offs_sb[:]))
-        nc.vector.tensor_copy(xw_g[0][:], xw[:].indirect(offs_sb[:, : HALF // 16]))
 
-        w_bf = sb.tile([P, PACK, P, PACK], BF16, name="w_bf", align_bytes=64)
+        w_bf = [sb.tile([P, 2, P, PACK], BF16, name=f"w_bf{u}", align_bytes=64) for u in range(2)]
 
-        def deal(raw, first, lo, hi):
-            dealt = w_bf[:, :, lo:hi, :].rearrange("p t m j -> p m t j")
-            source = raw[:, :, PACK * (lo - first) : PACK * (hi - first)].rearrange("p j (m t) -> p m t j", t=PACK)
+        def deal(u, lo, hi):
+            dealt = w_bf[u][:, :, lo:hi, :].rearrange("p t m j -> p m t j")
+            source = w_raw[:, :, PACK * lo : PACK * hi].rearrange("p j (m t) -> p m t j", t=PACK)[:, :, 2 * u : 2 * u + 2, :]
             return dealt, source
 
-        nc.scalar.activation(*deal(w_first, 0, 0, W_FIRST), COPY)
-        nc.vector.tensor_copy(*deal(w_rest, W_FIRST, W_FIRST, W_FIRST + W_VECTOR))
-        nc.scalar.activation(*deal(w_rest, W_FIRST, W_FIRST + W_VECTOR, P), COPY)
         w_codes = [sb.tile([P, P], U32, name=f"w_codes{t}", align_bytes=64) for t in range(PACK)]
         w_scales = [sb.tile([P, P], U8, name=f"w_scales{t}", align_bytes=64) for t in range(PACK)]
 
-        def product(t, h):
-            lo, hi = halves[h]
+        def product(t, lo, hi, bank):
             nc.tensor.matmul_mx(
-                out=first_bank[:] if (t, h) == (0, 0) else banks[t][:, lo:hi],
+                out=bank,
                 lhsT=w_codes[t][:].bitcast(FP8X4),
                 lhsT_scale=w_scales[t][:],
-                rhs=xw_g[h][:].bitcast(FP8X4),
+                rhs=xw_g[:, lo:hi].bitcast(FP8X4),
                 rhs_scale=xs_g[:, lo:hi],
                 start=True,
                 stop=True,
             )
 
         for t in range(PACK):
-            nc.vector.quantize_mx(out=w_codes[t][:].bitcast(FP8X4), scales=w_scales[t][:], in_=w_bf[:, t, :, :].rearrange("p m j -> p (m j)"))
-            product(t, 0)
-        xw_g.append(sb.tile([P, HALF], U32, name="xw_g1", tag="w_rest", align_bytes=64))
-        nc.vector.tensor_copy(xw_g[1][:], xw[:].indirect(offs_sb[:, HALF // 16 :]))
-        for t in range(PACK):
-            product(t, 1)
+            if t % 2 == 0:
+                nc.vector.tensor_copy(*deal(t // 2, 0, W_VECTOR[t // 2]))
+                nc.scalar.activation(*deal(t // 2, W_VECTOR[t // 2], P), COPY)
+            nc.vector.quantize_mx(out=w_codes[t][:].bitcast(FP8X4), scales=w_scales[t][:], in_=w_bf[t // 2][:, t % 2, :, :].rearrange("p m j -> p (m j)"))
+            if t == 0:
+                product(t, 0, HALF, first_bank[:])
+                product(t, HALF, S, banks[t][:, HALF:])
+            else:
+                product(t, 0, S, banks[t][:])
 
         def places(t, lo, hi):
             return win[t][:].indirect(slot_sb[:, lo // 16 : hi // 16])
@@ -122,11 +115,15 @@ def tile_picked_ema_none_po_kernel(tc, x_words, x_scales, mem, w1, old, new, off
             kept = sb.tile([P, S], F32, name=f"kept{t}", align_bytes=64)
             parts = ((0, S),)
             if t == 0:
-                for h, (lo, hi) in enumerate(halves):
-                    nc.vector.tensor_tensor(kept[:, lo:hi], picked[h][:], old_sb[:, lo:hi], MULT)
-                    nc.vector.tensor_tensor(fresh[0][:, lo:hi], first_bank[:] if h == 0 else banks[0][:, lo:hi], new_sb[:, lo:hi], MULT)
-                    nc.vector.tensor_tensor(z[:, lo:hi], kept[:, lo:hi], fresh[0][:, lo:hi], ADD)
+                fresh_first = sb.tile([P, HALF], F32, name="fresh_first", tag="first", align_bytes=64)
+                nc.vector.tensor_tensor(fresh_first[:], first_bank[:], new_sb[:, :HALF], MULT)
+                nc.vector.tensor_tensor(kept[:, :HALF], picked[0][:], old_sb[:, :HALF], MULT)
+                nc.vector.tensor_tensor(fresh[0][:, HALF:], banks[0][:, HALF:], new_sb[:, HALF:], MULT)
+                nc.vector.tensor_tensor(z[:, :HALF], kept[:, :HALF], fresh_first[:], ADD)
+                kept_second = sb.tile([P, HALF], F32, name="kept_second", tag="first", align_bytes=64)
+                nc.vector.tensor_tensor(kept_second[:], picked[1][:], old_sb[:, HALF:], MULT)
                 weigh_new(1)
+                nc.vector.tensor_tensor(z[:, HALF:], kept_second[:], fresh[0][:, HALF:], ADD)
                 parts = ()
             elif t == 1:
                 for lo, hi in halves:

@@ -19,6 +19,8 @@ COPY = mybir.ActivationFunctionType.Copy
 P = 128
 PACK = 4
 HALF = S // 2
+OWN = 96
+MID = 288
 W_VECTOR = (76, 64)
 PIECES = ((0, 256, "scalar"), (256, 512, "vector"), (512, 704, "scalar"), (704, 1024, "vector"))
 QUANT = ((256, 512), (0, 256), (768, 1024), (512, 768))
@@ -50,8 +52,7 @@ def tile_picked_ema_none_po_kernel(tc, x_words, x_scales, mem, w1, old, new, off
         nc.sync.dma_start(offs_sb[:], offs)
         nc.sync.dma_start(slot_sb[:], slot)
         for q in range(4):
-            queue = nc.sync if q < 2 else nc.scalar
-            queue.dma_start(xs[32 * q : 32 * q + 4, :].bitcast(I32), x_scales[0, 4 * q : 4 * q + 4, :].bitcast(I32))
+            nc.sync.dma_start(xs[32 * q : 32 * q + 4, :].bitcast(I32), x_scales[0, 4 * q : 4 * q + 4, :].bitcast(I32))
         nc.sync.dma_start(w_raw[:], w_rows)
         nc.sync.dma_start(win[0][:], mem_rows[:, 0, :])
         for lo, hi in halves:
@@ -68,34 +69,35 @@ def tile_picked_ema_none_po_kernel(tc, x_words, x_scales, mem, w1, old, new, off
         w_bf = [sb.tile([P, 2, P, PACK], BF16, name=f"w_bf{u}", align_bytes=64) for u in range(2)]
 
         def deal(u, lo, hi):
-            dealt = w_bf[u][:, :, lo:hi, :].rearrange("p t m j -> p m t j")
-            source = w_raw[:, :, PACK * lo : PACK * hi].rearrange("p j (m t) -> p m t j", t=PACK)[:, :, 2 * u : 2 * u + 2, :]
+            dealt = w_bf[u][:, :, lo:hi, :].rearrange("p t m j -> p m j t")
+            source = w_raw[:, :, PACK * lo : PACK * hi].rearrange("p j (m t) -> p m j t", t=PACK)[:, :, :, 2 * u : 2 * u + 2]
             return dealt, source
 
-        w_codes = [sb.tile([P, P], U32, name=f"w_codes{t}", align_bytes=64) for t in range(PACK)]
-        w_scales = [sb.tile([P, P], U8, name=f"w_scales{t}", align_bytes=64) for t in range(PACK)]
+        w_codes = [sb.tile([P, 2 * P], U32, name=f"w_codes{u}", align_bytes=64) for u in range(2)]
+        w_scales = [sb.tile([P, 2 * P], U8, name=f"w_scales{u}", align_bytes=64) for u in range(2)]
 
         def product(t, lo, hi, bank):
+            cols = slice(t % 2 * P, (t % 2 + 1) * P)
             nc.tensor.matmul_mx(
                 out=bank,
-                lhsT=w_codes[t][:].bitcast(FP8X4),
-                lhsT_scale=w_scales[t][:],
+                lhsT=w_codes[t // 2][:, cols].bitcast(FP8X4),
+                lhsT_scale=w_scales[t // 2][:, cols],
                 rhs=xw_g[:, lo:hi].bitcast(FP8X4),
                 rhs_scale=xs_g[:, lo:hi],
                 start=True,
                 stop=True,
             )
 
-        for t in range(PACK):
-            if t % 2 == 0:
-                nc.vector.tensor_copy(*deal(t // 2, 0, W_VECTOR[t // 2]))
-                nc.scalar.activation(*deal(t // 2, W_VECTOR[t // 2], P), COPY)
-            nc.vector.quantize_mx(out=w_codes[t][:].bitcast(FP8X4), scales=w_scales[t][:], in_=w_bf[t // 2][:, t % 2, :, :].rearrange("p m j -> p (m j)"))
-            if t == 0:
-                product(t, 0, HALF, first_bank[:])
-                product(t, HALF, S, banks[t][:, HALF:])
-            else:
-                product(t, 0, S, banks[t][:])
+        for u in range(2):
+            nc.vector.tensor_copy(*deal(u, 0, W_VECTOR[u]))
+            nc.scalar.activation(*deal(u, W_VECTOR[u], P), COPY)
+            nc.vector.quantize_mx(out=w_codes[u][:].bitcast(FP8X4), scales=w_scales[u][:], in_=w_bf[u][:].rearrange("p t m j -> p (t m j)"))
+            for t in (2 * u, 2 * u + 1):
+                if t == 0:
+                    product(t, 0, HALF, first_bank[:])
+                    product(t, HALF, S, banks[t][:, HALF:])
+                else:
+                    product(t, 0, S, banks[t][:])
 
         def places(t, lo, hi):
             return win[t][:].indirect(slot_sb[:, lo // 16 : hi // 16])
@@ -112,7 +114,7 @@ def tile_picked_ema_none_po_kernel(tc, x_words, x_scales, mem, w1, old, new, off
         for t in range(PACK):
             last = t == PACK - 1
             z = None if last else sb.tile([P, S], F32, name=f"z{t}", align_bytes=64)
-            kept = sb.tile([P, S], F32, name=f"kept{t}", align_bytes=64)
+            kept = kept_last if last else sb.tile([P, S], F32, name=f"kept{t}", align_bytes=64)
             parts = ((0, S),)
             if t == 0:
                 fresh_first = sb.tile([P, HALF], F32, name="fresh_first", tag="first", align_bytes=64)
@@ -130,18 +132,24 @@ def tile_picked_ema_none_po_kernel(tc, x_words, x_scales, mem, w1, old, new, off
                     nc.vector.tensor_tensor(kept[:, lo:hi], places(t, lo, hi), old_sb[:, lo:hi], MULT)
                 nc.vector.tensor_tensor(z[:, :HALF], kept[:, :HALF], fresh[t][:, :HALF], ADD)
                 parts = ((HALF, S),)
-            else:
+            elif t == 2:
                 nc.vector.tensor_tensor(kept[:], places(t, 0, S), old_sb[:], MULT)
             if t in (1, 2):
                 weigh_new(t + 1)
-            own = (0, 0, 0, S)[t]
+            if t == 2:
+                nc.vector.tensor_tensor(z[:, OWN:MID], kept[:, OWN:MID], fresh[t][:, OWN:MID], ADD)
+                nc.vector.tensor_tensor(places(t, 0, OWN), kept[:, :OWN], fresh[t][:, :OWN], ADD)
+                kept_last = sb.tile([P, S], F32, name="kept_last", align_bytes=64)
+                nc.vector.tensor_tensor(kept_last[:], places(t + 1, 0, S), old_sb[:], MULT)
+                parts = ((MID, S),)
+            own = (0, 0, OWN, S)[t]
             if not last:
                 for lo, hi in parts:
                     nc.vector.tensor_tensor(z[:, lo:hi], kept[:, lo:hi], fresh[t][:, lo:hi], ADD)
-            if own:
+            if last:
                 nc.vector.tensor_tensor(places(t, 0, own), kept[:, :own], fresh[t][:, :own], ADD)
             if not last:
-                for lo, hi in ((own, own + (S - own) // 2), (own + (S - own) // 2, S)):
+                for lo, hi in ((OWN, MID), (MID, S)) if own else halves:
                     nc.scalar.activation(places(t, lo, hi), z[:, lo:hi], COPY)
             for h in range(2):
                 columns = win[t][:, h * U // 2 : (h + 1) * U // 2]

@@ -19,8 +19,7 @@ COPY = mybir.ActivationFunctionType.Copy
 P = 128
 PACK = 4
 HALF = S // 2
-OWN = 96
-MID = 288
+SHORT = 128
 W_VECTOR = (76, 64)
 PIECES = ((0, 256, "scalar"), (256, 512, "vector"), (512, 704, "scalar"), (704, 1024, "vector"))
 QUANT = ((256, 512), (0, 256), (768, 1024), (512, 768))
@@ -103,63 +102,68 @@ def tile_picked_ema_none_po_kernel(tc, x_words, x_scales, mem, w1, old, new, off
             return win[t][:].indirect(slot_sb[:, lo // 16 : hi // 16])
 
         planes = [sb.tile([P, PACK, U // 2], F32, name=f"planes{h}", align_bytes=64) for h in range(2)]
-        picked = [sb.tile([P, HALF], F32, name=f"picked{h}", align_bytes=64) for h in range(2)]
+        picked = [sb.tile([P, HALF], F32, name=f"picked{h}", tag=f"picked{h}", align_bytes=64) for h in range(2)]
         for h, (lo, hi) in enumerate(halves):
             nc.scalar.activation(picked[h][:], places(0, lo, hi), COPY)
-        fresh = [sb.tile([P, S], F32, name=f"fresh{t}", tag=f"fresh{t % 2}", align_bytes=64) for t in range(PACK)]
+        fresh = {}
+        kept = [sb.tile([P, S], F32, name=f"kept{t}", align_bytes=64) for t in range(PACK)]
+        z = [sb.tile([P, S], F32, name=f"z{t}", align_bytes=64) for t in range(PACK)]
 
         def weigh_new(t):
+            fresh[t] = sb.tile([P, S], F32, name=f"fresh{t}", tag=("fresh0", "fresh1", "fresh0", "first")[t], align_bytes=64)
             nc.vector.tensor_tensor(fresh[t][:], banks[t][:], new_sb[:], MULT)
 
-        for t in range(PACK):
-            last = t == PACK - 1
-            z = None if last else sb.tile([P, S], F32, name=f"z{t}", align_bytes=64)
-            kept = kept_last if last else sb.tile([P, S], F32, name=f"kept{t}", align_bytes=64)
-            parts = ((0, S),)
-            if t == 0:
-                fresh_first = sb.tile([P, HALF], F32, name="fresh_first", tag="first", align_bytes=64)
-                nc.vector.tensor_tensor(fresh_first[:], first_bank[:], new_sb[:, :HALF], MULT)
-                nc.vector.tensor_tensor(kept[:, :HALF], picked[0][:], old_sb[:, :HALF], MULT)
-                nc.vector.tensor_tensor(fresh[0][:, HALF:], banks[0][:, HALF:], new_sb[:, HALF:], MULT)
-                nc.vector.tensor_tensor(z[:, :HALF], kept[:, :HALF], fresh_first[:], ADD)
-                kept_second = sb.tile([P, HALF], F32, name="kept_second", tag="first", align_bytes=64)
-                nc.vector.tensor_tensor(kept_second[:], picked[1][:], old_sb[:, HALF:], MULT)
-                weigh_new(1)
-                nc.vector.tensor_tensor(z[:, HALF:], kept_second[:], fresh[0][:, HALF:], ADD)
-                parts = ()
-            elif t == 1:
-                for lo, hi in halves:
-                    nc.vector.tensor_tensor(kept[:, lo:hi], places(t, lo, hi), old_sb[:, lo:hi], MULT)
-                nc.vector.tensor_tensor(z[:, :HALF], kept[:, :HALF], fresh[t][:, :HALF], ADD)
-                parts = ((HALF, S),)
-            elif t == 2:
-                nc.vector.tensor_tensor(kept[:], places(t, 0, S), old_sb[:], MULT)
-            if t in (1, 2):
-                weigh_new(t + 1)
-            if t == 2:
-                nc.vector.tensor_tensor(z[:, OWN:MID], kept[:, OWN:MID], fresh[t][:, OWN:MID], ADD)
-                nc.vector.tensor_tensor(places(t, 0, OWN), kept[:, :OWN], fresh[t][:, :OWN], ADD)
-                kept_last = sb.tile([P, S], F32, name="kept_last", align_bytes=64)
-                nc.vector.tensor_tensor(kept_last[:], places(t + 1, 0, S), old_sb[:], MULT)
-                parts = ((MID, S),)
-            own = (0, 0, OWN, S)[t]
-            if not last:
-                for lo, hi in parts:
-                    nc.vector.tensor_tensor(z[:, lo:hi], kept[:, lo:hi], fresh[t][:, lo:hi], ADD)
-            if last:
-                nc.vector.tensor_tensor(places(t, 0, own), kept[:, :own], fresh[t][:, :own], ADD)
-            if not last:
-                for lo, hi in ((OWN, MID), (MID, S)) if own else halves:
-                    nc.scalar.activation(places(t, lo, hi), z[:, lo:hi], COPY)
-            for h in range(2):
-                columns = win[t][:, h * U // 2 : (h + 1) * U // 2]
-                if t < 2:
-                    nc.sync.dma_start(planes[h][:, t, :], columns)
-                elif last:
-                    nc.vector.tensor_copy(planes[h][:, t, :], columns)
-                else:
-                    nc.scalar.copy(planes[h][:, t, :], columns)
+        def weigh_old(t, lo, hi):
+            nc.vector.tensor_tensor(kept[t][:, lo:hi], places(t, lo, hi), old_sb[:, lo:hi], MULT)
+
+        def blend(t, lo, hi):
+            nc.vector.tensor_tensor(z[t][:, lo:hi], kept[t][:, lo:hi], fresh[t][:, lo:hi], ADD)
+
+        def put(t, lo, hi):
+            nc.scalar.activation(places(t, lo, hi), z[t][:, lo:hi], COPY)
+
+        def hand_on(t):
+            if t < 2:
+                for h in range(2):
+                    nc.sync.dma_start(planes[h][:, t, :], win[t][:, h * U // 2 : (h + 1) * U // 2])
             nc.sync.dma_start(out_rows[:, t, :], win[t][:])
+
+        fresh[0] = sb.tile([P, S], F32, name="fresh0", tag="fresh0", align_bytes=64)
+        fresh_first = sb.tile([P, HALF], F32, name="fresh_first", tag="first", align_bytes=64)
+        nc.vector.tensor_tensor(fresh_first[:], first_bank[:], new_sb[:, :HALF], MULT)
+        nc.vector.tensor_tensor(kept[0][:, :HALF], picked[0][:], old_sb[:, :HALF], MULT)
+        nc.vector.tensor_tensor(fresh[0][:, HALF:], banks[0][:, HALF:], new_sb[:, HALF:], MULT)
+        nc.vector.tensor_tensor(z[0][:, :HALF], kept[0][:, :HALF], fresh_first[:], ADD)
+        kept_second = sb.tile([P, HALF], F32, name="kept_second", tag="picked0", align_bytes=64)
+        nc.vector.tensor_tensor(kept_second[:], picked[1][:], old_sb[:, HALF:], MULT)
+        weigh_new(1)
+        nc.vector.tensor_tensor(z[0][:, HALF:], kept_second[:], fresh[0][:, HALF:], ADD)
+        for lo, hi in halves:
+            put(0, lo, hi)
+        hand_on(0)
+
+        for lo, hi in halves:
+            weigh_old(1, lo, hi)
+        weigh_new(2)
+        blend(1, 0, S - SHORT)
+        weigh_old(2, 0, S)
+        weigh_new(3)
+        blend(2, 0, SHORT)
+        blend(1, S - SHORT, S)
+        weigh_old(3, 0, S)
+        blend(2, SHORT, S)
+        put(1, 0, S - SHORT)
+        put(2, 0, SHORT)
+        put(1, S - SHORT, S)
+        put(2, SHORT, S)
+        hand_on(1)
+        nc.vector.tensor_tensor(places(3, 0, S), kept[3][:], fresh[3][:], ADD)
+        nc.vector.tensor_copy(planes[0][:, 2, :], win[2][:, : U // 2])
+        nc.scalar.copy(planes[1][:, 2, :], win[2][:, U // 2 :])
+        hand_on(2)
+        for h in range(2):
+            nc.vector.tensor_copy(planes[h][:, 3, :], win[3][:, h * U // 2 : (h + 1) * U // 2])
+        hand_on(3)
 
         o_scales = sb.tile([P, U], U8, name="o_scales", align_bytes=64)
         o_words = out_1[0].rearrange("p n t -> p (n t)").bitcast(I32)

@@ -21,7 +21,8 @@ PACK = 4
 HALF = S // 2
 SHORT = 128
 W_VECTOR = (76, 64)
-PIECES = ((0, 256, "scalar"), (256, 512, "vector"), (512, 704, "scalar"), (704, 1024, "vector"))
+GROUPS = ((0, 512), (512, 768), (768, 1024))
+PIECES = ((0, 224, "scalar"), (224, 512, "vector"), (512, 768, "scalar"), (768, 1024, "vector"))
 QUANT = ((256, 512), (0, 256), (768, 1024), (512, 768))
 
 
@@ -138,18 +139,21 @@ def tile_picked_ema_none_po_kernel(tc, x_words, x_scales, mem, w1, old, new, off
         nc.vector.tensor_tensor(kept_second[:], picked[1][:], old_sb[:, HALF:], MULT)
         weigh_new(1)
         nc.vector.tensor_tensor(z[0][:, HALF:], kept_second[:], fresh[0][:, HALF:], ADD)
-        for lo, hi in halves:
-            put(0, lo, hi)
+        picked_next = sb.tile([P, SHORT], F32, name="picked_next", align_bytes=64)
+        put(0, 0, HALF)
+        nc.scalar.activation(picked_next[:], places(1, S - SHORT, S), COPY)
+        put(0, HALF, S)
         hand_on(0)
 
-        for lo, hi in halves:
-            weigh_old(1, lo, hi)
+        weigh_old(1, 0, S - SHORT)
         weigh_new(2)
         blend(1, 0, S - SHORT)
+        kept_next = sb.tile([P, SHORT], F32, name="kept_next", tag="picked0", align_bytes=64)
+        nc.vector.tensor_tensor(kept_next[:], picked_next[:], old_sb[:, S - SHORT :], MULT)
         weigh_old(2, 0, S)
         weigh_new(3)
         blend(2, 0, SHORT)
-        blend(1, S - SHORT, S)
+        nc.vector.tensor_tensor(z[1][:, S - SHORT :], kept_next[:], fresh[1][:, S - SHORT :], ADD)
         weigh_old(3, 0, S)
         blend(2, SHORT, S)
         put(1, 0, S - SHORT)
@@ -167,21 +171,23 @@ def tile_picked_ema_none_po_kernel(tc, x_words, x_scales, mem, w1, old, new, off
 
         o_scales = sb.tile([P, U], U8, name="o_scales", align_bytes=64)
         o_words = out_1[0].rearrange("p n t -> p (n t)").bitcast(I32)
-        grouped = [sb.tile([P, U // 2, PACK], BF16, name=f"grouped{h}", align_bytes=64) for h in range(2)]
+        grouped = {lo: sb.tile([P, hi - lo, PACK], BF16, name=f"grouped{lo}", align_bytes=64) for lo, hi in GROUPS}
+
+        def woven(lo, hi):
+            start = max(first for first, last in GROUPS if first <= lo)
+            return grouped[start][:, lo - start : hi - start, :]
+
         for lo, hi, engine in PIECES:
             h = lo // (U // 2)
-            cols = slice(lo - h * U // 2, hi - h * U // 2)
-            source = planes[h][:, :, cols].rearrange("p t (c i) -> p c t i", i=4)
-            woven = grouped[h][:, cols, :].rearrange("p (c i) t -> p c t i", i=4)
+            source = planes[h][:, :, lo - h * U // 2 : hi - h * U // 2].rearrange("p t (c i) -> p c t i", i=4)
+            target = woven(lo, hi).rearrange("p (c i) t -> p c t i", i=4)
             if engine == "vector":
-                nc.vector.tensor_copy(woven, source)
+                nc.vector.tensor_copy(target, source)
             else:
-                nc.scalar.activation(woven, source, COPY)
+                nc.scalar.activation(target, source, COPY)
         for lo, hi in QUANT:
-            h = lo // (U // 2)
-            cols = slice(lo - h * U // 2, hi - h * U // 2)
             o_codes = sb.tile([P, hi - lo], U32, name=f"o_codes{lo}", align_bytes=64)
-            nc.vector.quantize_mx(out=o_codes[:].bitcast(FP8X4), scales=o_scales[:, lo:hi], in_=grouped[h][:, cols, :].rearrange("p c t -> p (c t)"))
+            nc.vector.quantize_mx(out=o_codes[:].bitcast(FP8X4), scales=o_scales[:, lo:hi], in_=woven(lo, hi).rearrange("p c t -> p (c t)"))
             nc.sync.dma_start(o_words[:, lo:hi], o_codes[:].bitcast(I32))
         for q in range(4):
             queue = nc.scalar if q < 2 else nc.sync

@@ -20,7 +20,7 @@ P = 128
 PACK = 4
 HALF = S // 2
 SHORT = 128
-W_VECTOR = (76, 64)
+W_VECTOR = (88, 80)
 GROUPS = ((0, 512), (512, 768), (768, 1024))
 PIECES = ((0, 224, "scalar"), (224, 512, "vector"), (512, 768, "scalar"), (768, 1024, "vector"))
 QUANT = ((256, 512), (0, 256), (768, 1024), (512, 768))

from contextlib import ExitStack

import concourse.mybir as mybir

K, T, S, N, U = 512, 1024, 512, 512, 1024
FLOPS = 2 * K * N * S

F32 = mybir.dt.float32
BF16 = mybir.dt.bfloat16
I32 = mybir.dt.int32
U32 = mybir.dt.uint32
U16 = mybir.dt.uint16
U8 = mybir.dt.uint8
FP8X4 = mybir.dt.float8_e4m3fn_x4
MULT = mybir.AluOpType.mult
ADD = mybir.AluOpType.add
COPY = mybir.ActivationFunctionType.Copy

P = 128
PACK = 4
HALF = S // 2
SHORT = 128
W_VECTOR = (88, 80)
GROUPS = ((0, 512), (512, 768), (768, 1024))
PIECES = ((0, 224, "scalar"), (224, 512, "vector"), (512, 768, "scalar"), (768, 1024, "vector"))
QUANT = ((256, 512), (0, 256), (768, 1024), (512, 768))


def tile_picked_ema_none_po_kernel(tc, x_words, x_scales, mem, w1, old, new, offs, slot, out_0, out_1, out_2):
    nc = tc.nc
    with ExitStack() as ctx:
        sb = ctx.enter_context(tc.tile_pool(name="sb", bufs=1))
        ps = ctx.enter_context(tc.psum_pool(name="ps", bufs=1))

        offs_sb = sb.tile([P, S // 16], U16, name="offs_sb")
        slot_sb = sb.tile([P, S // 16], U16, name="slot_sb")
        xw = sb.tile([P, T], U32, name="xw", align_bytes=64)
        xs = sb.tile([P, T], U8, name="xs", align_bytes=64)
        w_raw = sb.tile([P, PACK, N], F32, name="w_raw", align_bytes=64)
        old_sb = sb.tile([P, S], F32, name="old_sb", align_bytes=64)
        new_sb = sb.tile([P, S], F32, name="new_sb", align_bytes=64)
        halves = ((0, HALF), (HALF, S))
        win = [sb.tile([P, U], F32, name=f"win{t}", align_bytes=64) for t in range(PACK)]
        banks = [ps.tile([P, S], F32, name=f"bank{t}") for t in range(PACK)]
        first_bank = ps.tile([P, HALF], F32, name="first_bank")

        nc.vector.memset(xs[:].bitcast(I32), 0)
        w_rows = w1.rearrange("(p j) c -> p j c", j=PACK)
        mem_rows = mem.rearrange("(p t) c -> p t c", t=PACK)
        out_rows = out_0.rearrange("(p t) c -> p t c", t=PACK)
        nc.sync.dma_start(xw[:].bitcast(I32), x_words[0].rearrange("p n t -> p (n t)").bitcast(I32))
        nc.sync.dma_start(offs_sb[:], offs)
        nc.sync.dma_start(slot_sb[:], slot)
        for q in range(4):
            nc.sync.dma_start(xs[32 * q : 32 * q + 4, :].bitcast(I32), x_scales[0, 4 * q : 4 * q + 4, :].bitcast(I32))
        nc.sync.dma_start(w_raw[:], w_rows)
        nc.sync.dma_start(win[0][:], mem_rows[:, 0, :])
        for lo, hi in halves:
            nc.sync.dma_start(new_sb[:, lo:hi], new[:, lo:hi])
            nc.sync.dma_start(old_sb[:, lo:hi], old[:, lo:hi])
        for t in range(1, PACK):
            nc.sync.dma_start(win[t][:], mem_rows[:, t, :])

        xs_g = sb.tile([P, S], U8, name="xs_g", align_bytes=64)
        xw_g = sb.tile([P, S], U32, name="xw_g", align_bytes=64)
        nc.vector.tensor_copy(xw_g[:], xw[:].indirect(offs_sb[:]))
        nc.vector.tensor_copy(xs_g[:], xs[:].indirect(offs_sb[:]))

        w_bf = [sb.tile([P, 2, P, PACK], BF16, name=f"w_bf{u}", align_bytes=64) for u in range(2)]

        def deal(u, lo, hi):
            dealt = w_bf[u][:, :, lo:hi, :].rearrange("p t m j -> p m j t")
            source = w_raw[:, :, PACK * lo : PACK * hi].rearrange("p j (m t) -> p m j t", t=PACK)[:, :, :, 2 * u : 2 * u + 2]
            return dealt, source

        w_codes = [sb.tile([P, 2 * P], U32, name=f"w_codes{u}", align_bytes=64) for u in range(2)]
        w_scales = [sb.tile([P, 2 * P], U8, name=f"w_scales{u}", align_bytes=64) for u in range(2)]

        def product(t, lo, hi, bank):
            cols = slice(t % 2 * P, (t % 2 + 1) * P)
            nc.tensor.matmul_mx(
                out=bank,
                lhsT=w_codes[t // 2][:, cols].bitcast(FP8X4),
                lhsT_scale=w_scales[t // 2][:, cols],
                rhs=xw_g[:, lo:hi].bitcast(FP8X4),
                rhs_scale=xs_g[:, lo:hi],
                start=True,
                stop=True,
            )

        for u in range(2):
            nc.vector.tensor_copy(*deal(u, 0, W_VECTOR[u]))
            nc.scalar.activation(*deal(u, W_VECTOR[u], P), COPY)
            nc.vector.quantize_mx(out=w_codes[u][:].bitcast(FP8X4), scales=w_scales[u][:], in_=w_bf[u][:].rearrange("p t m j -> p (t m j)"))
            for t in (2 * u, 2 * u + 1):
                if t == 0:
                    product(t, 0, HALF, first_bank[:])
                    product(t, HALF, S, banks[t][:, HALF:])
                else:
                    product(t, 0, S, banks[t][:])

        def places(t, lo, hi):
            return win[t][:].indirect(slot_sb[:, lo // 16 : hi // 16])

        planes = [sb.tile([P, PACK, U // 2], F32, name=f"planes{h}", align_bytes=64) for h in range(2)]
        picked = [sb.tile([P, HALF], F32, name=f"picked{h}", tag=f"picked{h}", align_bytes=64) for h in range(2)]
        for h, (lo, hi) in enumerate(halves):
            nc.scalar.activation(picked[h][:], places(0, lo, hi), COPY)
        fresh = {}
        kept = [sb.tile([P, S], F32, name=f"kept{t}", align_bytes=64) for t in range(PACK)]
        z = [sb.tile([P, S], F32, name=f"z{t}", align_bytes=64) for t in range(PACK)]

        def weigh_new(t):
            fresh[t] = sb.tile([P, S], F32, name=f"fresh{t}", tag=("fresh0", "fresh1", "fresh0", "first")[t], align_bytes=64)
            nc.vector.tensor_tensor(fresh[t][:], banks[t][:], new_sb[:], MULT)

        def weigh_old(t, lo, hi):
            nc.vector.tensor_tensor(kept[t][:, lo:hi], places(t, lo, hi), old_sb[:, lo:hi], MULT)

        def blend(t, lo, hi):
            nc.vector.tensor_tensor(z[t][:, lo:hi], kept[t][:, lo:hi], fresh[t][:, lo:hi], ADD)

        def put(t, lo, hi):
            nc.scalar.activation(places(t, lo, hi), z[t][:, lo:hi], COPY)

        def hand_on(t):
            if t < 2:
                for h in range(2):
                    nc.sync.dma_start(planes[h][:, t, :], win[t][:, h * U // 2 : (h + 1) * U // 2])
            nc.sync.dma_start(out_rows[:, t, :], win[t][:])

        fresh[0] = sb.tile([P, S], F32, name="fresh0", tag="fresh0", align_bytes=64)
        fresh_first = sb.tile([P, HALF], F32, name="fresh_first", tag="first", align_bytes=64)
        nc.vector.tensor_tensor(fresh_first[:], first_bank[:], new_sb[:, :HALF], MULT)
        nc.vector.tensor_tensor(kept[0][:, :HALF], picked[0][:], old_sb[:, :HALF], MULT)
        nc.vector.tensor_tensor(fresh[0][:, HALF:], banks[0][:, HALF:], new_sb[:, HALF:], MULT)
        nc.vector.tensor_tensor(z[0][:, :HALF], kept[0][:, :HALF], fresh_first[:], ADD)
        kept_second = sb.tile([P, HALF], F32, name="kept_second", tag="picked0", align_bytes=64)
        nc.vector.tensor_tensor(kept_second[:], picked[1][:], old_sb[:, HALF:], MULT)
        weigh_new(1)
        nc.vector.tensor_tensor(z[0][:, HALF:], kept_second[:], fresh[0][:, HALF:], ADD)
        picked_next = sb.tile([P, SHORT], F32, name="picked_next", align_bytes=64)
        put(0, 0, HALF)
        nc.scalar.activation(picked_next[:], places(1, S - SHORT, S), COPY)
        put(0, HALF, S)
        hand_on(0)

        weigh_old(1, 0, S - SHORT)
        weigh_new(2)
        blend(1, 0, S - SHORT)
        kept_next = sb.tile([P, SHORT], F32, name="kept_next", tag="picked0", align_bytes=64)
        nc.vector.tensor_tensor(kept_next[:], picked_next[:], old_sb[:, S - SHORT :], MULT)
        weigh_old(2, 0, S)
        weigh_new(3)
        blend(2, 0, SHORT)
        nc.vector.tensor_tensor(z[1][:, S - SHORT :], kept_next[:], fresh[1][:, S - SHORT :], ADD)
        weigh_old(3, 0, S)
        blend(2, SHORT, S)
        put(1, 0, S - SHORT)
        put(2, 0, SHORT)
        put(1, S - SHORT, S)
        put(2, SHORT, S)
        hand_on(1)
        nc.vector.tensor_tensor(places(3, 0, S), kept[3][:], fresh[3][:], ADD)
        nc.vector.tensor_copy(planes[0][:, 2, :], win[2][:, : U // 2])
        nc.scalar.copy(planes[1][:, 2, :], win[2][:, U // 2 :])
        hand_on(2)
        for h in range(2):
            nc.vector.tensor_copy(planes[h][:, 3, :], win[3][:, h * U // 2 : (h + 1) * U // 2])
        hand_on(3)

        o_scales = sb.tile([P, U], U8, name="o_scales", align_bytes=64)
        o_words = out_1[0].rearrange("p n t -> p (n t)").bitcast(I32)
        grouped = {lo: sb.tile([P, hi - lo, PACK], BF16, name=f"grouped{lo}", align_bytes=64) for lo, hi in GROUPS}

        def woven(lo, hi):
            start = max(first for first, last in GROUPS if first <= lo)
            return grouped[start][:, lo - start : hi - start, :]

        for lo, hi, engine in PIECES:
            h = lo // (U // 2)
            source = planes[h][:, :, lo - h * U // 2 : hi - h * U // 2].rearrange("p t (c i) -> p c t i", i=4)
            target = woven(lo, hi).rearrange("p (c i) t -> p c t i", i=4)
            if engine == "vector":
                nc.vector.tensor_copy(target, source)
            else:
                nc.scalar.activation(target, source, COPY)
        for lo, hi in QUANT:
            o_codes = sb.tile([P, hi - lo], U32, name=f"o_codes{lo}", align_bytes=64)
            nc.vector.quantize_mx(out=o_codes[:].bitcast(FP8X4), scales=o_scales[:, lo:hi], in_=woven(lo, hi).rearrange("p c t -> p (c t)"))
            nc.sync.dma_start(o_words[:, lo:hi], o_codes[:].bitcast(I32))
        for q in range(4):
            queue = nc.scalar if q < 2 else nc.sync
            queue.dma_start(out_2[0, 4 * q : 4 * q + 4, :].bitcast(I32), o_scales[32 * q : 32 * q + 4, :].bitcast(I32))
